import numpy as np
CORES = [127,119,111,103,95,87,79,71,63,55,47,39,31,23,15,7]
N = 16
ROOT = 0
def setup_inputs(rng):
    return {"x": rng.standard_normal((N, 128, 128), dtype=np.float32)}
def reference(x):
    y = np.full((N, 128, N * 128), np.nan, x.dtype)
    y[ROOT] = np.concatenate(list(x), axis=1)
    return {"y": y}

@@ -1,0 +1,100 @@
+import comms_topo
+
+W = 128
+NR = 16
+ROOT = 127
+
+
+def core_at(chip, k):
+    return chip * 8 + k
+
+
+def chip_of_rank(j):
+    return 15 - j
+
+
+VIA = {}
+for jj in range(1, 8):
+    VIA[jj] = []
+for jj in range(8, 12):
+    VIA[jj] = [core_at(chip_of_rank(jj), 3)]
+VIA[12] = [core_at(14, 6)]
+VIA[13] = [core_at(14, 7)]
+VIA[14] = [core_at(14, 2)]
+VIA[15] = [core_at(14, 3)]
+
+GROUPS = [(1, 7, "sync"), (8, 11, "scalar"), (12, 15, "sync")]
+
+NSLOT = 2
+
+SCRATCH = {
+    "land": ("sbuf", [128, NR * W], "float32"),
+    "stage": ("dram", [128, W], "float32"),
+    "hop": ("dram", [NSLOT, 128, W], "float32"),
+}
+SEMAPHORES = (["loaded", "sent", "stored"] + ["in%d" % s for s in range(NSLOT)]
+              + ["grp%d" % k for k in range(len(GROUPS))])
+
+
+def group_of(j):
+    for k, (a, b, qq) in enumerate(GROUPS):
+        if a <= j <= b:
+            return k
+    return None
+
+
+def plan():
+    slots = {}
+    sends = {}
+    for j in range(1, NR):
+        path = [core_at(chip_of_rank(j), 7)] + VIA[j] + [ROOT]
+        here = None
+        for a, b in zip(path[:-1], path[1:]):
+            there = None
+            if b != ROOT:
+                there = slots.get(b, 0)
+                slots[b] = there + 1
+            sends.setdefault(a, []).append((j, here, b, there))
+            here = there
+    for c in sends:
+        sends[c].sort(key=lambda s: 0 if s[1] is None else 1)
+    return sends
+
+
+def rank_program(g, core, T, topo):
+    if core == ROOT:
+        n = 1
+        g.scalar.dma_start(T.y[:, 0:W], T.x[:]).then_inc(T.sem.stored, 16)
+        for k, (a, b, q) in enumerate(GROUPS):
+            queue = g.sync if q == "sync" else g.scalar
+            queue.wait_ge(T.sem["grp%d" % k], 8 * (b - a + 1))
+            queue.dma_start(T.y[:, a * W:(b + 1) * W], T.land[:, a * W:(b + 1) * W]).then_inc(T.sem.stored, 16)
+            n += 1
+        g.wait_ge(T.sem.stored, 16 * n)
+        return
+
+    sends = plan().get(core)
+    if not sends:
+        return
+    if T.rank_of(core) is not None:
+        g.sync.dma_start(T.stage[:], T.x[:]).then_inc(T.sem.loaded, 16)
+    left = 0
+    for (j, here, nxt, there) in sends:
+        if here is None:
+            g.wait_ge(T.sem.loaded, 16)
+            src = T.stage[:]
+        else:
+            prev = ([core_at(chip_of_rank(j), 7)] + VIA[j])[VIA[j].index(core)]
+            g.wait_ge(T.sem["in%d" % here], 16 if topo.chip(prev) == topo.chip(core) else 8)
+            src = T.hop[here]
+        if nxt == ROOT:
+            dst = T.land[:, j * W:(j + 1) * W]
+            sem = T.sem["grp%d" % group_of(j)]
+        else:
+            dst = T.hop[there]
+            sem = T.sem["in%d" % there]
+        rid, pid, se = topo.addr(nxt)
+        mask = topo.mask(core, nxt)
+        g.remote_dma(dst, src, sem, T.sem.sent, pid, rid, mask)
+        left += 16 if mask == 0xFFFF else 8
+    g.wait_ge(T.sem.sent, left)

@@ -19,11 +19,13 @@ for jj in range(1, 8):
 for jj in range(8, 12):
     VIA[jj] = [core_at(chip_of_rank(jj), 3)]
 VIA[12] = [core_at(14, 6)]
-VIA[13] = [core_at(14, 7)]
-VIA[14] = [core_at(14, 2)]
-VIA[15] = [core_at(14, 3)]
+VIA[13] = [core_at(14, 2)]
+VIA[14] = [core_at(chip_of_rank(14), 3), core_at(14, 7)]
+VIA[15] = [core_at(chip_of_rank(15), 3), core_at(14, 3)]
 
-GROUPS = [(1, 7, "sync"), (8, 11, "scalar"), (12, 15, "sync")]
+PACE = {5: 2, 6: 3, 7: 4, 10: 8, 11: 9}
+
+GROUPS = [(1, 4, "sync"), (5, 7, "sync"), (8, 9, "scalar"), (10, 11, "scalar"), (14, 15, "scalar"), (12, 13, "g")]
 
 NSLOT = 2
 
@@ -32,7 +34,7 @@ SCRATCH = {
     "stage": ("dram", [128, W], "float32"),
     "hop": ("dram", [NSLOT, 128, W], "float32"),
 }
-SEMAPHORES = (["loaded", "sent", "stored"] + ["in%d" % s for s in range(NSLOT)]
+SEMAPHORES = (["loaded", "sent", "stored", "storedg", "go"] + ["in%d" % s for s in range(NSLOT)]
               + ["grp%d" % k for k in range(len(GROUPS))])
 
 
@@ -64,24 +66,35 @@ def plan():
 def rank_program(g, core, T, topo):
     if core == ROOT:
         n = 1
+        ng = 0
         g.scalar.dma_start(T.y[:, 0:W], T.x[:]).then_inc(T.sem.stored, 16)
         for k, (a, b, q) in enumerate(GROUPS):
-            queue = g.sync if q == "sync" else g.scalar
+            queue = g.sync if q == "sync" else (g.scalar if q == "scalar" else g)
             queue.wait_ge(T.sem["grp%d" % k], 8 * (b - a + 1))
-            queue.dma_start(T.y[:, a * W:(b + 1) * W], T.land[:, a * W:(b + 1) * W]).then_inc(T.sem.stored, 16)
-            n += 1
+            d = queue.dma_start(T.y[:, a * W:(b + 1) * W], T.land[:, a * W:(b + 1) * W])
+            if q == "g":
+                d.then_inc(T.sem.storedg, 16)
+                ng += 1
+            else:
+                d.then_inc(T.sem.stored, 16)
+                n += 1
+        if ng:
+            g.wait_ge(T.sem.storedg, 16 * ng)
         g.wait_ge(T.sem.stored, 16 * n)
         return
 
     sends = plan().get(core)
     if not sends:
         return
-    if T.rank_of(core) is not None:
+    me = T.rank_of(core)
+    if me is not None:
         g.sync.dma_start(T.stage[:], T.x[:]).then_inc(T.sem.loaded, 16)
     left = 0
     for (j, here, nxt, there) in sends:
         if here is None:
             g.wait_ge(T.sem.loaded, 16)
+            if me in PACE:
+                g.wait_ge(T.sem.go, 1)
             src = T.stage[:]
         else:
             prev = ([core_at(chip_of_rank(j), 7)] + VIA[j])[VIA[j].index(core)]
@@ -97,4 +110,10 @@ def rank_program(g, core, T, topo):
         mask = topo.mask(core, nxt)
         g.remote_dma(dst, src, sem, T.sem.sent, pid, rid, mask)
         left += 16 if mask == 0xFFFF else 8
+        if here is None:
+            for late, early in PACE.items():
+                if early == me:
+                    rid, pid, se = topo.addr(core_at(chip_of_rank(late), 7))
+                    g.remote_sem_update(T.sem.go, T.sem.sent, pid, rid, 0x1)
+                    left += 1
     g.wait_ge(T.sem.sent, left)

@@ -23,14 +23,18 @@ VIA[13] = [core_at(14, 2)]
 VIA[14] = [core_at(chip_of_rank(14), 3), core_at(14, 7)]
 VIA[15] = [core_at(chip_of_rank(15), 3), core_at(14, 3)]
 
-PACE = {5: 2, 6: 3, 7: 4, 10: 8, 11: 9}
+PACE = {6: 2, 7: 3}
 
-GROUPS = [(1, 4, "sync"), (5, 7, "sync"), (8, 9, "scalar"), (10, 11, "scalar"), (14, 15, "scalar"), (12, 13, "g")]
+DLAND = {1: 0, 14: 1, 15: 2}
+
+GROUPS = [(1, 1, "sync"), (2, 5, "sync"), (6, 7, "sync"), (15, 15, "sync"),
+          (8, 11, "scalar"), (14, 14, "scalar"), (12, 13, "g")]
 
 NSLOT = 2
 
 SCRATCH = {
     "land": ("sbuf", [128, NR * W], "float32"),
+    "dland": ("dram", [len(DLAND), 128, W], "float32"),
     "stage": ("dram", [128, W], "float32"),
     "hop": ("dram", [NSLOT, 128, W], "float32"),
 }
@@ -71,7 +75,8 @@ def rank_program(g, core, T, topo):
         for k, (a, b, q) in enumerate(GROUPS):
             queue = g.sync if q == "sync" else (g.scalar if q == "scalar" else g)
             queue.wait_ge(T.sem["grp%d" % k], 8 * (b - a + 1))
-            d = queue.dma_start(T.y[:, a * W:(b + 1) * W], T.land[:, a * W:(b + 1) * W])
+            src = T.dland[DLAND[a]] if a in DLAND else T.land[:, a * W:(b + 1) * W]
+            d = queue.dma_start(T.y[:, a * W:(b + 1) * W], src)
             if q == "g":
                 d.then_inc(T.sem.storedg, 16)
                 ng += 1
@@ -101,7 +106,7 @@ def rank_program(g, core, T, topo):
             g.wait_ge(T.sem["in%d" % here], 16 if topo.chip(prev) == topo.chip(core) else 8)
             src = T.hop[here]
         if nxt == ROOT:
-            dst = T.land[:, j * W:(j + 1) * W]
+            dst = T.dland[DLAND[j]] if j in DLAND else T.land[:, j * W:(j + 1) * W]
             sem = T.sem["grp%d" % group_of(j)]
         else:
             dst = T.hop[there]

import comms_topo

W = 128
NR = 16
ROOT = 127


def core_at(chip, k):
    return chip * 8 + k


def chip_of_rank(j):
    return 15 - j


VIA = {}
for jj in range(1, 8):
    VIA[jj] = []
for jj in range(8, 12):
    VIA[jj] = [core_at(chip_of_rank(jj), 3)]
VIA[12] = [core_at(14, 6)]
VIA[13] = [core_at(14, 2)]
VIA[14] = [core_at(chip_of_rank(14), 3), core_at(14, 7)]
VIA[15] = [core_at(chip_of_rank(15), 3), core_at(14, 3)]

PACE = {6: 2, 7: 3}

DLAND = {1: 0, 14: 1, 15: 2}

GROUPS = [(1, 1, "sync"), (2, 5, "sync"), (6, 7, "sync"), (15, 15, "sync"),
          (8, 11, "scalar"), (14, 14, "scalar"), (12, 13, "g")]

NSLOT = 2

SCRATCH = {
    "land": ("sbuf", [128, NR * W], "float32"),
    "dland": ("dram", [len(DLAND), 128, W], "float32"),
    "stage": ("dram", [128, W], "float32"),
    "hop": ("dram", [NSLOT, 128, W], "float32"),
}
SEMAPHORES = (["loaded", "sent", "stored", "storedg", "go"] + ["in%d" % s for s in range(NSLOT)]
              + ["grp%d" % k for k in range(len(GROUPS))])


def group_of(j):
    for k, (a, b, qq) in enumerate(GROUPS):
        if a <= j <= b:
            return k
    return None


def plan():
    slots = {}
    sends = {}
    for j in range(1, NR):
        path = [core_at(chip_of_rank(j), 7)] + VIA[j] + [ROOT]
        here = None
        for a, b in zip(path[:-1], path[1:]):
            there = None
            if b != ROOT:
                there = slots.get(b, 0)
                slots[b] = there + 1
            sends.setdefault(a, []).append((j, here, b, there))
            here = there
    for c in sends:
        sends[c].sort(key=lambda s: 0 if s[1] is None else 1)
    return sends


def rank_program(g, core, T, topo):
    if core == ROOT:
        n = 1
        ng = 0
        g.scalar.dma_start(T.y[:, 0:W], T.x[:]).then_inc(T.sem.stored, 16)
        for k, (a, b, q) in enumerate(GROUPS):
            queue = g.sync if q == "sync" else (g.scalar if q == "scalar" else g)
            queue.wait_ge(T.sem["grp%d" % k], 8 * (b - a + 1))
            src = T.dland[DLAND[a]] if a in DLAND else T.land[:, a * W:(b + 1) * W]
            d = queue.dma_start(T.y[:, a * W:(b + 1) * W], src)
            if q == "g":
                d.then_inc(T.sem.storedg, 16)
                ng += 1
            else:
                d.then_inc(T.sem.stored, 16)
                n += 1
        if ng:
            g.wait_ge(T.sem.storedg, 16 * ng)
        g.wait_ge(T.sem.stored, 16 * n)
        return

    sends = plan().get(core)
    if not sends:
        return
    me = T.rank_of(core)
    if me is not None:
        g.sync.dma_start(T.stage[:], T.x[:]).then_inc(T.sem.loaded, 16)
    left = 0
    for (j, here, nxt, there) in sends:
        if here is None:
            g.wait_ge(T.sem.loaded, 16)
            if me in PACE:
                g.wait_ge(T.sem.go, 1)
            src = T.stage[:]
        else:
            prev = ([core_at(chip_of_rank(j), 7)] + VIA[j])[VIA[j].index(core)]
            g.wait_ge(T.sem["in%d" % here], 16 if topo.chip(prev) == topo.chip(core) else 8)
            src = T.hop[here]
        if nxt == ROOT:
            dst = T.dland[DLAND[j]] if j in DLAND else T.land[:, j * W:(j + 1) * W]
            sem = T.sem["grp%d" % group_of(j)]
        else:
            dst = T.hop[there]
            sem = T.sem["in%d" % there]
        rid, pid, se = topo.addr(nxt)
        mask = topo.mask(core, nxt)
        g.remote_dma(dst, src, sem, T.sem.sent, pid, rid, mask)
        left += 16 if mask == 0xFFFF else 8
        if here is None:
            for late, early in PACE.items():
                if early == me:
                    rid, pid, se = topo.addr(core_at(chip_of_rank(late), 7))
                    g.remote_sem_update(T.sem.go, T.sem.sent, pid, rid, 0x1)
                    left += 1
    g.wait_ge(T.sem.sent, left)
